import numpy as np
import ml_dtypes


def mxq(x, axis, fmt="e4m3"):
    dtype, down = {"e4m3": (ml_dtypes.float8_e4m3fn, 7), "e5m2": (ml_dtypes.float8_e5m2, 14)}[fmt]
    v = np.moveaxis(np.asarray(x, np.float32).astype(ml_dtypes.bfloat16).astype(np.float64), axis, -1)
    blocks = v.reshape(v.shape[:-1] + (-1, 32))
    amax = np.abs(blocks).max(-1, keepdims=True)
    byte = np.maximum(np.where(amax > 0, np.frexp(amax)[1] - 1 + 127, 0) - down, 1)
    scale = np.exp2(byte - 127.0)
    codes = (blocks / scale).astype(np.float32).astype(dtype).astype(np.float64)
    return np.moveaxis((codes * scale).reshape(v.shape), -1, axis)


WIDE = False


def mx_kscale(k):
    if not WIDE:
        return np.ones(k)
    levels = np.array([30, -30])
    if k % 512:
        return np.exp2(np.random.permutation(np.resize(levels, k // 32))).repeat(32)
    a = np.empty((k // 512, 16))
    for p in range(k // 512):
        a[p, :8] = np.random.permutation(np.resize(levels, 8))
        for g in range(8):
            far = levels[np.abs(levels - a[p, g]) >= 10]
            a[p, g + 8] = far[np.random.randint(len(far))]
    return np.exp2(a.ravel()).repeat(32)


def f64(x):
    return np.asarray(x).astype(np.float64)


def striped(idx):
    return np.tile(idx.reshape(-1, 16).T, (8, 1)).astype(np.uint16)


def unstriped(offs):
    return offs[:16].T.reshape(-1).astype(np.int64)


E2M1 = np.array([0.0, 0.5, 1.0, 1.5, 2.0, 3.0, 4.0, 6.0, -0.0, -0.5, -1.0, -1.5, -2.0, -3.0, -4.0, -6.0])


def pack_weight(w, fmt):
    k, n = w.shape
    w = f64(np.asarray(w, np.float32).astype(ml_dtypes.bfloat16)).reshape(k // 32, 32, n)
    amax = np.abs(w).max(1)
    if fmt == "e4m3":
        byte = np.frexp(amax)[1] - 1 + 127 - 7
    elif fmt == "e5m2":
        byte = np.frexp(amax)[1] - 1 + 127 - 14
    else:
        mant, ex = np.frexp(amax / 6.0)
        byte = np.where(mant > 0.5, ex, ex - 1) + 127
    byte = np.clip(np.where(amax > 0, byte, 1), 1, 254)
    scaled = (w * np.exp2(127.0 - byte)[:, None, :]).reshape(k, n).astype(np.float32)
    by_word = np.ascontiguousarray(scaled.reshape(k // 512, 128, 4, n).transpose(0, 1, 3, 2))
    if fmt == "e4m3":
        words = by_word.astype(ml_dtypes.float8_e4m3fn).view(np.uint8)
    elif fmt == "e5m2":
        words = by_word.astype(ml_dtypes.float8_e5m2).view(np.uint8)
    else:
        c = by_word.astype(ml_dtypes.float4_e2m1fn).view(np.uint8) & 0xF
        words = (c[..., 0::2] | (c[..., 1::2] << 4)).reshape(k // 512, 128, 2 * n)
    return np.ascontiguousarray(words), np.ascontiguousarray(byte.astype(np.uint8).reshape(k // 512, 16, n))


def unpack_weight(words, scales, fmt):
    g, _, n = scales.shape
    words = np.ascontiguousarray(words).reshape(g, 128, n, -1)
    if fmt == "e4m3":
        vals = words.view(ml_dtypes.float8_e4m3fn).astype(np.float64)
    elif fmt == "e5m2":
        vals = words.view(ml_dtypes.float8_e5m2).astype(np.float64)
    else:
        nib = np.empty((g, 128, n, 4), np.uint8)
        nib[..., 0::2] = words & 0xF
        nib[..., 1::2] = words >> 4
        vals = E2M1[nib]
    vals = vals * np.repeat(np.exp2(scales.astype(np.float64) - 127.0), 8, axis=1)[..., None]
    return vals.transpose(0, 1, 3, 2).reshape(g * 512, n)


def d_relu2(v):
    return 2.0 * np.maximum(v, 0.0)


K, T, E, C, H, N = 256, 1536, 6, 512, 1024, 512


def by_expert(wq, xq):
    return np.concatenate([wq[e].T @ xq[:, e * C:(e + 1) * C] for e in range(E)], axis=1)


def setup_inputs():
    n = np.random.standard_normal
    s = mx_kscale(N)[:, None]
    u = mx_kscale(H)
    first = np.random.permutation(np.repeat(np.arange(E), T // E))
    second = (first + 1 + np.random.permutation(np.repeat(np.arange(E - 1), -(-T // (E - 1)))[:T])) % E
    while np.bincount(second, minlength=E).max() != T // E:
        load = np.bincount(second, minlength=E); hi, lo = int(load.argmax()), int(load.argmin())
        t = np.flatnonzero((second == hi) & (first != lo))[0]; second[t] = lo
    slot_token = np.empty(E * C, np.int64); pos = np.empty((2, T), np.int64); fill = np.zeros(E, np.int64)
    place = np.stack([np.random.permutation(C) for _ in range(E)])
    for r, deal in enumerate((first, second)):
        for t in np.random.permutation(T):
            e = deal[t]; j = e * C + place[e, fill[e]]; fill[e] += 1; slot_token[j] = t; pos[r, t] = j
    g = np.random.uniform(0.2, 0.8, T)
    w_slot = np.empty(E * C); w_slot[pos[0]] = g; w_slot[pos[1]] = 1.0 - g
    dy = pack_weight(n((N, T)) * s, "e5m2")
    w2 = [pack_weight(m, "e2m1") for m in n((E, N, H)) / np.sqrt(N) / s[None] * u[None, None, :]]
    w1 = [pack_weight(m, "e2m1") for m in n((E, H, K)) / np.sqrt(H) / u[None, :, None]]
    return {
        "dy_words": dy[0],
        "dy_scales": dy[1],
        "a": n((H, E * C)).astype(np.float32),
        "w2_words": np.stack([m[0] for m in w2]),
        "w2_scales": np.stack([m[1] for m in w2]),
        "w1_words": np.stack([m[0] for m in w1]),
        "w1_scales": np.stack([m[1] for m in w1]),
        "gate": np.tile(w_slot, (H, 1)).astype(np.float32),
        "offs": striped(slot_token),
        "pos1": striped(pos[0]),
        "pos2": striped(pos[1]),
    }


def reference(dy_words, dy_scales, a, w2_words, w2_scales, w1_words, w1_scales, gate, offs, pos1, pos2):
    idx = unstriped(offs)
    w2 = np.stack([unpack_weight(w2_words[e], w2_scales[e], "e2m1") for e in range(E)])
    w1 = np.stack([unpack_weight(w1_words[e], w1_scales[e], "e2m1") for e in range(E)])
    gq = unpack_weight(dy_words, dy_scales, "e5m2")[:, idx]
    dh = f64(gate) * by_expert(w2, gq)
    da = dh * d_relu2(f64(a))
    dx = by_expert(w1, mxq(da, 0, "e5m2"))
    return dx[:, unstriped(pos1)] + dx[:, unstriped(pos2)]

@@ -1,0 +1,215 @@
+from contextlib import ExitStack
+
+import concourse.mybir as mybir
+from concourse.masks import make_identity
+
+K, T, E, C, H, N = 256, 1536, 6, 512, 1024, 512
+S = E * C
+
+FLOPS = 2 * S * (N * H + H * K)
+BYTES = (
+    4 * H * S + 4 * S + 4 * K * T + N * T + N * T // 32
+    + E * (N * H + H * K) // 2 + E * (N * H + H * K) // 32 + 128 * 2 * (S + 2 * T) // 16
+)
+
+F32 = mybir.dt.float32
+BF16 = mybir.dt.bfloat16
+I32 = mybir.dt.int32
+U32 = mybir.dt.uint32
+U16 = mybir.dt.uint16
+U8 = mybir.dt.uint8
+E5M2 = mybir.dt.float8_e5m2_x4
+E2M1 = mybir.dt.float4_e2m1fn_x4
+ALU = mybir.AluOpType
+COPY = mybir.ActivationFunctionType.Copy
+
+P = 128
+PACK = 4
+PASS = P * PACK
+PASSES = H // PASS
+BLOCKS = S // P
+UNIT = 256
+UNITS = S // UNIT
+K_TILES = K // P
+PIECE = 512
+LANES = 16
+
+
+def tile_moe_bdx_mlp_relu2_kernel(
+    tc, dy_words, dy_scales, a, w2_words, w2_scales, w1_words, w1_scales, gate, offs, pos1, pos2, out
+):
+    nc = tc.nc
+    with ExitStack() as ctx:
+        keep = ctx.enter_context(tc.tile_pool(name="keep", bufs=1))
+        gathered = ctx.enter_context(tc.tile_pool(name="gathered", bufs=3))
+        gated = ctx.enter_context(tc.tile_pool(name="gated", bufs=4))
+        rounded = ctx.enter_context(tc.tile_pool(name="rounded", bufs=3))
+        coded = ctx.enter_context(tc.tile_pool(name="coded", bufs=2))
+        combine = ctx.enter_context(tc.tile_pool(name="combine", bufs=3))
+        psum_sums = ctx.enter_context(tc.psum_pool(name="psum_sums", bufs=3))
+        psum_turned = ctx.enter_context(tc.psum_pool(name="psum_turned", bufs=3))
+        psum_dx = ctx.enter_context(tc.psum_pool(name="psum_dx", bufs=2))
+
+        offs_sb = keep.tile([P, S // LANES], U16, name="offs_sb")
+        pos_sb = [keep.tile([P, T // LANES], U16, name="pos%d_sb" % (r + 1)) for r in range(2)]
+        dy_w = keep.tile([P, T], I32, name="dy_w", align_bytes=64)
+        dy_s = keep.tile([P, T], U8, name="dy_s", align_bytes=64)
+        w2_w = [keep.tile([P, 2 * H], U8, name="w2_w%d" % e, align_bytes=64) for e in range(E)]
+        w2_s = keep.tile([P, E, H], U8, name="w2_s", align_bytes=64)
+        w1_w = keep.tile([P, E * PASSES, 2 * K], U8, name="w1_w", align_bytes=64)
+        w1_s = keep.tile([P, E * PASSES, K], U8, name="w1_s", align_bytes=64)
+        gate_rows = keep.tile([P, P], F32, name="gate_rows")
+        gate2 = keep.tile([P, BLOCKS], F32, name="gate2")
+        ident = keep.tile([P, P], F32, name="ident")
+        dx = [keep.tile([P, S], F32, name="dx%d" % kt) for kt in range(K_TILES)]
+        a_sb = {}
+
+        nc.vector.memset(dy_s[:].bitcast(I32), 0)
+        nc.vector.memset(w2_s[:].rearrange("p e i -> p (e i)").bitcast(I32), 0)
+        make_identity(nc, ident[:])
+        nc.gpsimd.memset(w1_s[:].rearrange("p g k -> p (g k)").bitcast(I32), 0)
+
+        def load_scales(plane, rows):
+            for r in range(4):
+                nc.sync.dma_start(out=plane[r:P:32].bitcast(I32), in_=rows[r:16:4].bitcast(I32))
+
+        def load_a(first, width, s):
+            tile = keep.tile([P, PACK, width], F32, name="a_%d_%d" % (first, s))
+            rows = a[s * PASS : (s + 1) * PASS, first : first + width]
+            nc.sync.dma_start(out=tile[:], in_=rows.rearrange("(p t) j -> p t j", t=PACK))
+            for j in range(first // P, (first + width) // P):
+                a_sb[j, s] = tile[:, :, j * P - first : (j + 1) * P - first]
+
+        def load_w2(e):
+            nc.sync.dma_start(out=w2_w[e][:].bitcast(I32), in_=w2_words[e, 0].bitcast(I32))
+
+        nc.sync.dma_start(offs_sb[:], offs)
+        nc.sync.dma_start(out=dy_w[:], in_=dy_words[0].rearrange("p t d -> p (t d)").bitcast(I32))
+        load_scales(dy_s[:], dy_scales[0])
+        load_scales(w2_s[:], w2_scales.rearrange("e s f i -> f (e s) i"))
+        nc.sync.dma_start(out=gate_rows[:], in_=gate.rearrange("h (c q) -> (h c) q", q=P)[0:P])
+        load_w2(0)
+        for first in (0, UNIT):
+            for s in range(PASSES):
+                load_a(first, UNIT, s)
+        for e in range(1, E):
+            load_w2(e)
+            for s in range(PASSES):
+                load_a(e * C, C, s)
+            if e == 1:
+                load_scales(w1_s[:], w1_scales.rearrange("e s f k -> f (e s) k"))
+                nc.sync.dma_start(
+                    out=w1_w[:].bitcast(I32), in_=w1_words.rearrange("e s p c -> p (e s) c").bitcast(I32)
+                )
+        nc.sync.dma_start(pos_sb[0][:], pos1)
+        nc.sync.dma_start(pos_sb[1][:], pos2)
+
+        gate_turned = psum_turned.tile([P, PACK, P], F32, name="turned")
+        nc.tensor.transpose(gate_turned[:, 0, :], gate_rows[:], ident[:])
+        nc.scalar.activation(out=gate2[:], in_=gate_turned[:, 0, 0:BLOCKS], func=COPY, scale=2.0)
+
+        g_w, g_s, dh_t, da, codes, scales = {}, {}, {}, {}, {}, {}
+
+        def gather_dy(u):
+            entries = offs_sb[:, u * UNIT // LANES : (u + 1) * UNIT // LANES]
+            g_w[u] = gathered.tile([P, UNIT], U32, name="g_w", align_bytes=64)
+            g_s[u] = gathered.tile([P, UNIT], U8, name="g_s", align_bytes=64)
+            nc.vector.tensor_copy(g_w[u][:], dy_w[:].bitcast(U32).indirect(entries))
+            nc.vector.tensor_copy(g_s[u][:], dy_s[:].indirect(entries))
+
+        def first_product(j):
+            e, u = j * P // C, j * P // UNIT
+            slots = slice(j * P % UNIT, j * P % UNIT + P)
+            for s in range(PASSES):
+                sums = psum_sums.tile([P, PASS], F32, name="sums")
+                nc.tensor.matmul_mx(
+                    out=sums[:],
+                    lhsT=g_w[u][:, slots].bitcast(E5M2),
+                    lhsT_scale=g_s[u][:, slots],
+                    rhs=w2_w[e][:, 2 * s * PASS : 2 * (s + 1) * PASS].bitcast(E2M1),
+                    rhs_scale=w2_s[:, e, s * PASS : (s + 1) * PASS],
+                    start=True,
+                    stop=True,
+                )
+                dh_t[j, s] = gated.tile([P, PACK, P], F32, name="dh_t")
+                nc.scalar.activation(
+                    out=dh_t[j, s][:],
+                    in_=sums[:].rearrange("p (m t) -> p t m", t=PACK),
+                    func=COPY,
+                    scale=gate2[:, j : j + 1],
+                )
+
+        def turn_and_multiply(j):
+            u = j * P // UNIT
+            slots = slice(j * P % UNIT, j * P % UNIT + P)
+            if u not in da:
+                da[u] = rounded.tile([P, PASSES, UNIT, PACK], BF16, name="da", align_bytes=64)
+            for s in range(PASSES):
+                turned = psum_turned.tile([P, PACK, P], F32, name="turned")
+                for t in range(PACK):
+                    nc.tensor.transpose(turned[:, t, :], dh_t[j, s][:, t, :], ident[:])
+                nc.vector.scalar_tensor_tensor(
+                    out=da[u][:, s, slots, :],
+                    in0=a_sb[j, s].rearrange("p t n -> p n t"),
+                    scalar=0.0,
+                    in1=turned[:].rearrange("p t n -> p n t"),
+                    op0=ALU.max,
+                    op1=ALU.mult,
+                )
+
+        def quantize(u):
+            e = u * UNIT // C
+            slots = slice(u * UNIT % C, u * UNIT % C + UNIT)
+            if e not in codes:
+                codes[e] = coded.tile([P, PASSES, C], U32, name="codes", align_bytes=64)
+                scales[e] = coded.tile([P, PASSES, C], U8, name="scales", align_bytes=64)
+            for s in range(PASSES):
+                nc.vector.quantize_mx(
+                    out=codes[e][:, s, slots].bitcast(E5M2),
+                    scales=scales[e][:, s, slots],
+                    in_=da[u][:, s].rearrange("p n t -> p (n t)"),
+                )
+
+        def second_product(e):
+            for kt in range(K_TILES):
+                acc = psum_dx.tile([P, C], F32, name="acc")
+                for s in range(PASSES):
+                    g = e * PASSES + s
+                    nc.tensor.matmul_mx(
+                        out=acc[:],
+                        lhsT=w1_w[:, g, 2 * kt * P : 2 * (kt + 1) * P].bitcast(E2M1),
+                        lhsT_scale=w1_s[:, g, kt * P : (kt + 1) * P],
+                        rhs=codes[e][:, s, :].bitcast(E5M2),
+                        rhs_scale=scales[e][:, s, :],
+                        start=(s == 0),
+                        stop=(s == PASSES - 1),
+                    )
+                nc.scalar.copy(out=dx[kt][:, e * C : (e + 1) * C], in_=acc[:])
+
+        gather_dy(0)
+        gather_dy(1)
+        first_product(0)
+        for j in range(BLOCKS):
+            if j % 2 == 0 and j // 2 + 2 < UNITS:
+                gather_dy(j // 2 + 2)
+            if j % 4 == 1 and j > 4:
+                second_product(j // 4 - 1)
+            if j + 1 < BLOCKS:
+                first_product(j + 1)
+            turn_and_multiply(j)
+            if j % 2 == 0 and j > 0:
+                quantize(j // 2 - 1)
+        quantize(UNITS - 1)
+        second_product(E - 1)
+
+        for kt in range(K_TILES):
+            for first in range(0, T, PIECE):
+                picked = []
+                for r in range(2):
+                    one = combine.tile([P, PIECE], F32, name="picked%d" % r)
+                    entries = pos_sb[r][:, first // LANES : (first + PIECE) // LANES]
+                    nc.vector.tensor_copy(one[:], dx[kt][:].indirect(entries))
+                    picked.append(one)
+                total = combine.tile([P, PIECE], F32, name="total")
+                nc.vector.tensor_tensor(total[:], picked[0][:], picked[1][:], ALU.add)
+                nc.sync.dma_start(out=out[kt * P : (kt + 1) * P, first : first + PIECE], in_=total[:])

@@ -31,7 +31,6 @@ BLOCKS = S // P
 UNIT = 256
 UNITS = S // UNIT
 K_TILES = K // P
-PIECE = 512
 LANES = 16
 
 
@@ -42,7 +41,7 @@ def tile_moe_bdx_mlp_relu2_kernel(
     with ExitStack() as ctx:
         keep = ctx.enter_context(tc.tile_pool(name="keep", bufs=1))
         gathered = ctx.enter_context(tc.tile_pool(name="gathered", bufs=3))
-        gated = ctx.enter_context(tc.tile_pool(name="gated", bufs=4))
+        gated = ctx.enter_context(tc.tile_pool(name="gated", bufs=6))
         rounded = ctx.enter_context(tc.tile_pool(name="rounded", bufs=3))
         coded = ctx.enter_context(tc.tile_pool(name="coded", bufs=2))
         combine = ctx.enter_context(tc.tile_pool(name="combine", bufs=3))
@@ -69,26 +68,26 @@ def tile_moe_bdx_mlp_relu2_kernel(
         make_identity(nc, ident[:])
         nc.gpsimd.memset(w1_s[:].rearrange("p g k -> p (g k)").bitcast(I32), 0)
 
-        def load_scales(plane, rows):
+        def load_scales(queue, plane, rows):
             for r in range(4):
-                nc.sync.dma_start(out=plane[r:P:32].bitcast(I32), in_=rows[r:16:4].bitcast(I32))
+                queue.dma_start(out=plane[r:P:32].bitcast(I32), in_=rows[r:16:4].bitcast(I32))
 
         def load_a(first, width, s):
             tile = keep.tile([P, PACK, width], F32, name="a_%d_%d" % (first, s))
             rows = a[s * PASS : (s + 1) * PASS, first : first + width]
             nc.sync.dma_start(out=tile[:], in_=rows.rearrange("(p t) j -> p t j", t=PACK))
-            for j in range(first // P, (first + width) // P):
-                a_sb[j, s] = tile[:, :, j * P - first : (j + 1) * P - first]
+            for u in range(first // UNIT, (first + width) // UNIT):
+                a_sb[u, s] = tile[:, :, u * UNIT - first : (u + 1) * UNIT - first]
 
         def load_w2(e):
             nc.sync.dma_start(out=w2_w[e][:].bitcast(I32), in_=w2_words[e, 0].bitcast(I32))
 
         nc.sync.dma_start(offs_sb[:], offs)
         nc.sync.dma_start(out=dy_w[:], in_=dy_words[0].rearrange("p t d -> p (t d)").bitcast(I32))
-        load_scales(dy_s[:], dy_scales[0])
-        load_scales(w2_s[:], w2_scales.rearrange("e s f i -> f (e s) i"))
+        load_scales(nc.sync, dy_s[:], dy_scales[0])
         nc.sync.dma_start(out=gate_rows[:], in_=gate.rearrange("h (c q) -> (h c) q", q=P)[0:P])
         load_w2(0)
+        load_scales(nc.sync, w2_s[:], w2_scales.rearrange("e s f i -> f (e s) i"))
         for first in (0, UNIT):
             for s in range(PASSES):
                 load_a(first, UNIT, s)
@@ -97,18 +96,18 @@ def tile_moe_bdx_mlp_relu2_kernel(
             for s in range(PASSES):
                 load_a(e * C, C, s)
             if e == 1:
-                load_scales(w1_s[:], w1_scales.rearrange("e s f k -> f (e s) k"))
+                load_scales(nc.sync, w1_s[:], w1_scales.rearrange("e s f k -> f (e s) k"))
                 nc.sync.dma_start(
                     out=w1_w[:].bitcast(I32), in_=w1_words.rearrange("e s p c -> p (e s) c").bitcast(I32)
                 )
         nc.sync.dma_start(pos_sb[0][:], pos1)
         nc.sync.dma_start(pos_sb[1][:], pos2)
 
-        gate_turned = psum_turned.tile([P, PACK, P], F32, name="turned")
-        nc.tensor.transpose(gate_turned[:, 0, :], gate_rows[:], ident[:])
+        gate_turned = psum_turned.tile([P, 2, UNIT], F32, name="turned")
+        nc.tensor.transpose(gate_turned[:, 0, 0:P], gate_rows[:], ident[:])
         nc.scalar.activation(out=gate2[:], in_=gate_turned[:, 0, 0:BLOCKS], func=COPY, scale=2.0)
 
-        g_w, g_s, dh_t, da, codes, scales = {}, {}, {}, {}, {}, {}
+        g_w, g_s, dh_t, pairs, da, codes, scales = {}, {}, {}, {}, {}, {}, {}
 
         def gather_dy(u):
             entries = offs_sb[:, u * UNIT // LANES : (u + 1) * UNIT // LANES]
@@ -117,10 +116,12 @@ def tile_moe_bdx_mlp_relu2_kernel(
             nc.vector.tensor_copy(g_w[u][:], dy_w[:].bitcast(U32).indirect(entries))
             nc.vector.tensor_copy(g_s[u][:], dy_s[:].indirect(entries))
 
-        def first_product(j):
-            e, u = j * P // C, j * P // UNIT
-            slots = slice(j * P % UNIT, j * P % UNIT + P)
-            for s in range(PASSES):
+        def first_product(step):
+            u, s = divmod(step, PASSES)
+            e = u * UNIT // C
+            for b in range(UNIT // P):
+                slots = slice(b * P, (b + 1) * P)
+                j = u * UNIT // P + b
                 sums = psum_sums.tile([P, PASS], F32, name="sums")
                 nc.tensor.matmul_mx(
                     out=sums[:],
@@ -131,44 +132,50 @@ def tile_moe_bdx_mlp_relu2_kernel(
                     start=True,
                     stop=True,
                 )
-                dh_t[j, s] = gated.tile([P, PACK, P], F32, name="dh_t")
+                dh_t[step, b] = gated.tile([P, PACK, P], F32, name="dh_t")
                 nc.scalar.activation(
-                    out=dh_t[j, s][:],
+                    out=dh_t[step, b][:],
                     in_=sums[:].rearrange("p (m t) -> p t m", t=PACK),
                     func=COPY,
                     scale=gate2[:, j : j + 1],
                 )
 
-        def turn_and_multiply(j):
-            u = j * P // UNIT
-            slots = slice(j * P % UNIT, j * P % UNIT + P)
-            if u not in da:
-                da[u] = rounded.tile([P, PASSES, UNIT, PACK], BF16, name="da", align_bytes=64)
-            for s in range(PASSES):
-                turned = psum_turned.tile([P, PACK, P], F32, name="turned")
-                for t in range(PACK):
-                    nc.tensor.transpose(turned[:, t, :], dh_t[j, s][:, t, :], ident[:])
+        def turn_and_multiply(step):
+            u, s = divmod(step, PASSES)
+            pairs[step] = rounded.tile([P, 2, UNIT, 2], BF16, name="pairs", align_bytes=64)
+            for half in range(2):
+                turned = psum_turned.tile([P, 2, UNIT], F32, name="turned")
+                for b in range(UNIT // P):
+                    for d in range(2):
+                        nc.tensor.transpose(
+                            turned[:, d, b * P : (b + 1) * P], dh_t[step, b][:, 2 * half + d, :], ident[:]
+                        )
                 nc.vector.scalar_tensor_tensor(
-                    out=da[u][:, s, slots, :],
-                    in0=a_sb[j, s].rearrange("p t n -> p n t"),
+                    out=pairs[step][:, half],
+                    in0=a_sb[u, s][:, 2 * half : 2 * half + 2, :].rearrange("p d n -> p n d"),
                     scalar=0.0,
-                    in1=turned[:].rearrange("p t n -> p n t"),
+                    in1=turned[:].rearrange("p d n -> p n d"),
                     op0=ALU.max,
                     op1=ALU.mult,
                 )
 
-        def quantize(u):
+        def interleave(step):
+            da[step] = rounded.tile([P, UNIT * PACK], BF16, name="da", align_bytes=64)
+            nc.scalar.copy(
+                out=da[step][:].bitcast(F32).rearrange("p (n h) -> p n h", h=2),
+                in_=pairs[step][:].rearrange("p h n d -> p h (n d)").bitcast(F32).rearrange("p h n -> p n h"),
+            )
+
+        def quantize(step):
+            u, s = divmod(step, PASSES)
             e = u * UNIT // C
             slots = slice(u * UNIT % C, u * UNIT % C + UNIT)
             if e not in codes:
                 codes[e] = coded.tile([P, PASSES, C], U32, name="codes", align_bytes=64)
                 scales[e] = coded.tile([P, PASSES, C], U8, name="scales", align_bytes=64)
-            for s in range(PASSES):
-                nc.vector.quantize_mx(
-                    out=codes[e][:, s, slots].bitcast(E5M2),
-                    scales=scales[e][:, s, slots],
-                    in_=da[u][:, s].rearrange("p n t -> p (n t)"),
-                )
+            nc.vector.quantize_mx(
+                out=codes[e][:, s, slots].bitcast(E5M2), scales=scales[e][:, s, slots], in_=da[step][:]
+            )
 
         def second_product(e):
             for kt in range(K_TILES):
@@ -186,30 +193,43 @@ def tile_moe_bdx_mlp_relu2_kernel(
                     )
                 nc.scalar.copy(out=dx[kt][:, e * C : (e + 1) * C], in_=acc[:])
 
+        steps = UNITS * PASSES
+        per_expert = steps // E
         gather_dy(0)
         gather_dy(1)
         first_product(0)
-        for j in range(BLOCKS):
-            if j % 2 == 0 and j // 2 + 2 < UNITS:
-                gather_dy(j // 2 + 2)
-            if j % 4 == 1 and j > 4:
-                second_product(j // 4 - 1)
-            if j + 1 < BLOCKS:
-                first_product(j + 1)
-            turn_and_multiply(j)
-            if j % 2 == 0 and j > 0:
-                quantize(j // 2 - 1)
-        quantize(UNITS - 1)
-        second_product(E - 1)
+        for step in range(steps + 3):
+            if step % PASSES == 0 and step // PASSES + 2 < UNITS:
+                gather_dy(step // PASSES + 2)
+            if step > per_expert and (step - 2) % per_expert == 0:
+                second_product((step - 2) // per_expert - 1)
+            if step + 1 < steps:
+                first_product(step + 1)
+            if 0 <= step - 1 < steps:
+                interleave(step - 1)
+            if step < steps:
+                turn_and_multiply(step)
+            if 0 <= step - 1 < steps:
+                quantize(step - 1)
 
-        for kt in range(K_TILES):
-            for first in range(0, T, PIECE):
-                picked = []
-                for r in range(2):
-                    one = combine.tile([P, PIECE], F32, name="picked%d" % r)
-                    entries = pos_sb[r][:, first // LANES : (first + PIECE) // LANES]
-                    nc.vector.tensor_copy(one[:], dx[kt][:].indirect(entries))
-                    picked.append(one)
-                total = combine.tile([P, PIECE], F32, name="total")
-                nc.vector.tensor_tensor(total[:], picked[0][:], picked[1][:], ALU.add)
-                nc.sync.dma_start(out=out[kt * P : (kt + 1) * P, first : first + PIECE], in_=total[:])
+        pieces = [(kt, first, width) for kt in range(K_TILES) for first, width in ((0, 768), (768, 384), (1152, 384))]
+        picked = {}
+
+        def pick(n, r):
+            kt, first, width = pieces[n]
+            picked[n, r] = combine.tile([P, width], F32, name="picked%d" % r)
+            entries = pos_sb[r][:, first // LANES : (first + width) // LANES]
+            nc.vector.tensor_copy(picked[n, r][:], dx[kt][:].indirect(entries))
+
+        def add_and_store(n):
+            kt, first, width = pieces[n]
+            total = combine.tile([P, width], F32, name="total")
+            nc.vector.tensor_tensor(total[:], picked[n, 0][:], picked[n, 1][:], ALU.add)
+            nc.sync.dma_start(out=out[kt * P : (kt + 1) * P, first : first + width], in_=total[:])
+
+        for n in range(len(pieces)):
+            pick(n, 0)
+            if n > 0:
+                add_and_store(n - 1)
+            pick(n, 1)
+        add_and_store(len(pieces) - 1)

@@ -30,6 +30,8 @@ PASSES = H // PASS
 BLOCKS = S // P
 UNIT = 256
 UNITS = S // UNIT
+AHEAD = 2
+DIRECT_STEPS = 2
 K_TILES = K // P
 LANES = 16
 
@@ -41,20 +43,23 @@ def tile_moe_bdx_mlp_relu2_kernel(
     with ExitStack() as ctx:
         keep = ctx.enter_context(tc.tile_pool(name="keep", bufs=1))
         gathered = ctx.enter_context(tc.tile_pool(name="gathered", bufs=3))
+        paired = ctx.enter_context(tc.tile_pool(name="paired", bufs=3))
         gated = ctx.enter_context(tc.tile_pool(name="gated", bufs=6))
-        rounded = ctx.enter_context(tc.tile_pool(name="rounded", bufs=3))
+        rounded = ctx.enter_context(tc.tile_pool(name="rounded", bufs=4))
         coded = ctx.enter_context(tc.tile_pool(name="coded", bufs=2))
-        combine = ctx.enter_context(tc.tile_pool(name="combine", bufs=3))
+        combine = ctx.enter_context(tc.tile_pool(name="combine", bufs=2))
         psum_sums = ctx.enter_context(tc.psum_pool(name="psum_sums", bufs=3))
-        psum_turned = ctx.enter_context(tc.psum_pool(name="psum_turned", bufs=3))
-        psum_dx = ctx.enter_context(tc.psum_pool(name="psum_dx", bufs=2))
+        psum_turned = ctx.enter_context(tc.psum_pool(name="psum_turned", bufs=4))
+        psum_dx = ctx.enter_context(tc.psum_pool(name="psum_dx", bufs=1))
 
         offs_sb = keep.tile([P, S // LANES], U16, name="offs_sb")
         pos_sb = [keep.tile([P, T // LANES], U16, name="pos%d_sb" % (r + 1)) for r in range(2)]
         dy_w = keep.tile([P, T], I32, name="dy_w", align_bytes=64)
         dy_s = keep.tile([P, T], U8, name="dy_s", align_bytes=64)
         w2_w = [keep.tile([P, 2 * H], U8, name="w2_w%d" % e, align_bytes=64) for e in range(E)]
-        w2_s = keep.tile([P, E, H], U8, name="w2_s", align_bytes=64)
+        w2_s_first = keep.tile([P, 1, H], U8, name="w2_s_first", align_bytes=64)
+        w2_s_rest = keep.tile([P, E - 1, H], U8, name="w2_s_rest", align_bytes=64)
+        w2_s = [w2_s_first[:, 0, :]] + [w2_s_rest[:, e, :] for e in range(E - 1)]
         w1_w = keep.tile([P, E * PASSES, 2 * K], U8, name="w1_w", align_bytes=64)
         w1_s = keep.tile([P, E * PASSES, K], U8, name="w1_s", align_bytes=64)
         gate_rows = keep.tile([P, P], F32, name="gate_rows")
@@ -64,9 +69,8 @@ def tile_moe_bdx_mlp_relu2_kernel(
         a_sb = {}
 
         nc.vector.memset(dy_s[:].bitcast(I32), 0)
-        nc.vector.memset(w2_s[:].rearrange("p e i -> p (e i)").bitcast(I32), 0)
-        make_identity(nc, ident[:])
-        nc.gpsimd.memset(w1_s[:].rearrange("p g k -> p (g k)").bitcast(I32), 0)
+        for plane in (w2_s_first, w2_s_rest, w1_s):
+            nc.vector.memset(plane[:].rearrange("p g c -> p (g c)").bitcast(I32), 0)
 
         def load_scales(queue, plane, rows):
             for r in range(4):
@@ -79,20 +83,23 @@ def tile_moe_bdx_mlp_relu2_kernel(
             for u in range(first // UNIT, (first + width) // UNIT):
                 a_sb[u, s] = tile[:, :, u * UNIT - first : (u + 1) * UNIT - first]
 
-        def load_w2(e):
-            nc.sync.dma_start(out=w2_w[e][:].bitcast(I32), in_=w2_words[e, 0].bitcast(I32))
+        def load_w2(queue, e):
+            queue.dma_start(out=w2_w[e][:].bitcast(I32), in_=w2_words[e, 0].bitcast(I32))
 
         nc.sync.dma_start(offs_sb[:], offs)
         nc.sync.dma_start(out=dy_w[:], in_=dy_words[0].rearrange("p t d -> p (t d)").bitcast(I32))
         load_scales(nc.sync, dy_s[:], dy_scales[0])
+        w2_scale_rows = w2_scales.rearrange("e s f i -> f (e s) i")
         nc.sync.dma_start(out=gate_rows[:], in_=gate.rearrange("h (c q) -> (h c) q", q=P)[0:P])
-        load_w2(0)
-        load_scales(nc.sync, w2_s[:], w2_scales.rearrange("e s f i -> f (e s) i"))
+        load_w2(nc.sync, 0)
+        load_scales(nc.sync, w2_s_first[:], w2_scale_rows[:, 0:1])
+        make_identity(nc, ident[:])
         for first in (0, UNIT):
             for s in range(PASSES):
                 load_a(first, UNIT, s)
+        load_scales(nc.sync, w2_s_rest[:], w2_scale_rows[:, 1:E])
         for e in range(1, E):
-            load_w2(e)
+            load_w2(nc.sync, e)
             for s in range(PASSES):
                 load_a(e * C, C, s)
             if e == 1:
@@ -108,16 +115,21 @@ def tile_moe_bdx_mlp_relu2_kernel(
         nc.scalar.activation(out=gate2[:], in_=gate_turned[:, 0, 0:BLOCKS], func=COPY, scale=2.0)
 
         g_w, g_s, dh_t, pairs, da, codes, scales = {}, {}, {}, {}, {}, {}, {}
+        steps = [(u, s) for u in range(UNITS) for s in range(PASSES)]
+        steps_per_expert = len(steps) // E
 
-        def gather_dy(u):
-            entries = offs_sb[:, u * UNIT // LANES : (u + 1) * UNIT // LANES]
+        def gather_words(u):
             g_w[u] = gathered.tile([P, UNIT], U32, name="g_w", align_bytes=64)
-            g_s[u] = gathered.tile([P, UNIT], U8, name="g_s", align_bytes=64)
+            entries = offs_sb[:, u * UNIT // LANES : (u + 1) * UNIT // LANES]
             nc.vector.tensor_copy(g_w[u][:], dy_w[:].bitcast(U32).indirect(entries))
+
+        def gather_scales(u):
+            g_s[u] = gathered.tile([P, UNIT], U8, name="g_s", align_bytes=64)
+            entries = offs_sb[:, u * UNIT // LANES : (u + 1) * UNIT // LANES]
             nc.vector.tensor_copy(g_s[u][:], dy_s[:].indirect(entries))
 
-        def first_product(step):
-            u, s = divmod(step, PASSES)
+        def first_product(n):
+            u, s = steps[n]
             e = u * UNIT // C
             for b in range(UNIT // P):
                 slots = slice(b * P, (b + 1) * P)
@@ -128,91 +140,113 @@ def tile_moe_bdx_mlp_relu2_kernel(
                     lhsT=g_w[u][:, slots].bitcast(E5M2),
                     lhsT_scale=g_s[u][:, slots],
                     rhs=w2_w[e][:, 2 * s * PASS : 2 * (s + 1) * PASS].bitcast(E2M1),
-                    rhs_scale=w2_s[:, e, s * PASS : (s + 1) * PASS],
+                    rhs_scale=w2_s[e][:, s * PASS : (s + 1) * PASS],
                     start=True,
                     stop=True,
                 )
-                dh_t[step, b] = gated.tile([P, PACK, P], F32, name="dh_t")
+                dh_t[n, b] = gated.tile([P, PACK, P], F32, name="dh_t")
                 nc.scalar.activation(
-                    out=dh_t[step, b][:],
+                    out=dh_t[n, b][:],
                     in_=sums[:].rearrange("p (m t) -> p t m", t=PACK),
                     func=COPY,
                     scale=gate2[:, j : j + 1],
                 )
 
-        def turn_and_multiply(step):
-            u, s = divmod(step, PASSES)
-            pairs[step] = rounded.tile([P, 2, UNIT, 2], BF16, name="pairs", align_bytes=64)
-            for half in range(2):
-                turned = psum_turned.tile([P, 2, UNIT], F32, name="turned")
-                for b in range(UNIT // P):
-                    for d in range(2):
-                        nc.tensor.transpose(
-                            turned[:, d, b * P : (b + 1) * P], dh_t[step, b][:, 2 * half + d, :], ident[:]
-                        )
-                nc.vector.scalar_tensor_tensor(
-                    out=pairs[step][:, half],
-                    in0=a_sb[u, s][:, 2 * half : 2 * half + 2, :].rearrange("p d n -> p n d"),
-                    scalar=0.0,
-                    in1=turned[:].rearrange("p d n -> p n d"),
-                    op0=ALU.max,
-                    op1=ALU.mult,
-                )
-
-        def interleave(step):
-            da[step] = rounded.tile([P, UNIT * PACK], BF16, name="da", align_bytes=64)
-            nc.scalar.copy(
-                out=da[step][:].bitcast(F32).rearrange("p (n h) -> p n h", h=2),
-                in_=pairs[step][:].rearrange("p h n d -> p h (n d)").bitcast(F32).rearrange("p h n -> p n h"),
+        def relu_times(result, a_part, turned):
+            nc.vector.scalar_tensor_tensor(
+                out=result,
+                in0=a_part.rearrange("p t n -> p n t"),
+                scalar=0.0,
+                in1=turned.rearrange("p t n -> p n t"),
+                op0=ALU.max,
+                op1=ALU.mult,
             )
 
-        def quantize(step):
-            u, s = divmod(step, PASSES)
+        def multiply_pair(n, half):
+            if half == 0:
+                pairs[n] = paired.tile([P, 2, UNIT, 2], BF16, name="pairs", align_bytes=64)
+            turned = psum_turned.tile([P, 2, UNIT], F32, name="turned")
+            for b in range(UNIT // P):
+                for d in range(2):
+                    nc.tensor.transpose(turned[:, d, b * P : (b + 1) * P], dh_t[n, b][:, 2 * half + d, :], ident[:])
+            relu_times(pairs[n][:, half], a_sb[steps[n]][:, 2 * half : 2 * half + 2, :], turned[:])
+
+        def interleave(n):
+            da[n] = rounded.tile([P, UNIT * PACK], BF16, name="da", align_bytes=64)
+            copy = nc.vector.tensor_copy if n % 4 == 4-1 else nc.scalar.copy
+            copy(
+                out=da[n][:].bitcast(F32).rearrange("p (n h) -> p n h", h=2),
+                in_=pairs[n][:].rearrange("p h n d -> p h (n d)").bitcast(F32).rearrange("p h n -> p n h"),
+            )
+
+        def multiply_block(n, b):
+            if b == 0:
+                da[n] = rounded.tile([P, UNIT * PACK], BF16, name="da", align_bytes=64)
+            turned = psum_turned.tile([P, PACK, P], F32, name="turned")
+            for t in range(PACK):
+                nc.tensor.transpose(turned[:, t, :], dh_t[n, b][:, t, :], ident[:])
+            relu_times(
+                da[n][:, b * P * PACK : (b + 1) * P * PACK].rearrange("p (n t) -> p n t", t=PACK),
+                a_sb[steps[n]][:, :, b * P : (b + 1) * P],
+                turned[:],
+            )
+
+        def quantize(n, first, width):
+            u, s = steps[n]
             e = u * UNIT // C
-            slots = slice(u * UNIT % C, u * UNIT % C + UNIT)
             if e not in codes:
                 codes[e] = coded.tile([P, PASSES, C], U32, name="codes", align_bytes=64)
                 scales[e] = coded.tile([P, PASSES, C], U8, name="scales", align_bytes=64)
+            slots = slice(u * UNIT % C + first, u * UNIT % C + first + width)
             nc.vector.quantize_mx(
-                out=codes[e][:, s, slots].bitcast(E5M2), scales=scales[e][:, s, slots], in_=da[step][:]
+                out=codes[e][:, s, slots].bitcast(E5M2),
+                scales=scales[e][:, s, slots],
+                in_=da[n][:, first * PACK : (first + width) * PACK],
             )
 
-        def second_product(e):
-            for kt in range(K_TILES):
-                acc = psum_dx.tile([P, C], F32, name="acc")
-                for s in range(PASSES):
-                    g = e * PASSES + s
-                    nc.tensor.matmul_mx(
-                        out=acc[:],
-                        lhsT=w1_w[:, g, 2 * kt * P : 2 * (kt + 1) * P].bitcast(E2M1),
-                        lhsT_scale=w1_s[:, g, kt * P : (kt + 1) * P],
-                        rhs=codes[e][:, s, :].bitcast(E5M2),
-                        rhs_scale=scales[e][:, s, :],
-                        start=(s == 0),
-                        stop=(s == PASSES - 1),
-                    )
-                nc.scalar.copy(out=dx[kt][:, e * C : (e + 1) * C], in_=acc[:])
+        def second_product(e, kt):
+            acc = psum_dx.tile([P, C], F32, name="acc")
+            for s in range(PASSES):
+                g = e * PASSES + s
+                nc.tensor.matmul_mx(
+                    out=acc[:],
+                    lhsT=w1_w[:, g, 2 * kt * P : 2 * (kt + 1) * P].bitcast(E2M1),
+                    lhsT_scale=w1_s[:, g, kt * P : (kt + 1) * P],
+                    rhs=codes[e][:, s, :].bitcast(E5M2),
+                    rhs_scale=scales[e][:, s, :],
+                    start=(s == 0),
+                    stop=(s == PASSES - 1),
+                )
+            nc.scalar.copy(out=dx[kt][:, e * C : (e + 1) * C], in_=acc[:])
 
-        steps = UNITS * PASSES
-        per_expert = steps // E
-        gather_dy(0)
-        gather_dy(1)
+        last = len(steps) - 1
+        direct_from = len(steps) - DIRECT_STEPS
+        for u in range(AHEAD):
+            gather_words(u)
+            gather_scales(u)
         first_product(0)
-        for step in range(steps + 3):
-            if step % PASSES == 0 and step // PASSES + 2 < UNITS:
-                gather_dy(step // PASSES + 2)
-            if step > per_expert and (step - 2) % per_expert == 0:
-                second_product((step - 2) // per_expert - 1)
-            if step + 1 < steps:
-                first_product(step + 1)
-            if 0 <= step - 1 < steps:
-                interleave(step - 1)
-            if step < steps:
-                turn_and_multiply(step)
-            if 0 <= step - 1 < steps:
-                quantize(step - 1)
+        for n, (u, s) in enumerate(steps):
+            multiply = multiply_pair if n < direct_from else multiply_block
+            e, place = divmod(n, steps_per_expert)
+            if e > 0 and place >= 2:
+                second_product(e - 1, place - 2)
+            if n < last:
+                first_product(n + 1)
+            if 0 <= n - 1 < direct_from:
+                interleave(n - 1)
+            multiply(n, 0)
+            if u + AHEAD < UNITS:
+                (gather_words, gather_scales)[s](u + AHEAD)
+            multiply(n, 1)
+            if n >= 2:
+                quantize(n - 2, 0, UNIT)
+        quantize(last - 1, 0, UNIT)
+        for first in (0, P):
+            quantize(last, first, P)
+        for kt in range(K_TILES):
+            second_product(E - 1, kt)
 
-        pieces = [(kt, first, width) for kt in range(K_TILES) for first, width in ((0, 768), (768, 384), (1152, 384))]
+        pieces = [(0, 0, 768), (0, 768, 768), (1, 0, 768), (1, 768, 384), (1, 1152, 384)]
         picked = {}
 
         def pick(n, r):
@@ -224,7 +258,8 @@ def tile_moe_bdx_mlp_relu2_kernel(
         def add_and_store(n):
             kt, first, width = pieces[n]
             total = combine.tile([P, width], F32, name="total")
-            nc.vector.tensor_tensor(total[:], picked[n, 0][:], picked[n, 1][:], ALU.add)
+            engine = nc.vector if n == len(pieces) - 1 else nc.gpsimd
+            engine.tensor_tensor(total[:], picked[n, 0][:], picked[n, 1][:], ALU.add)
             nc.sync.dma_start(out=out[kt * P : (kt + 1) * P, first : first + width], in_=total[:])
 
         for n in range(len(pieces)):

@@ -43,11 +43,12 @@ def tile_moe_bdx_mlp_relu2_kernel(
     with ExitStack() as ctx:
         keep = ctx.enter_context(tc.tile_pool(name="keep", bufs=1))
         gathered = ctx.enter_context(tc.tile_pool(name="gathered", bufs=3))
-        paired = ctx.enter_context(tc.tile_pool(name="paired", bufs=3))
+        paired = ctx.enter_context(tc.tile_pool(name="paired", bufs=4))
         gated = ctx.enter_context(tc.tile_pool(name="gated", bufs=6))
         rounded = ctx.enter_context(tc.tile_pool(name="rounded", bufs=4))
-        coded = ctx.enter_context(tc.tile_pool(name="coded", bufs=2))
-        combine = ctx.enter_context(tc.tile_pool(name="combine", bufs=2))
+        coded = ctx.enter_context(tc.tile_pool(name="coded", bufs=E))
+        wide = ctx.enter_context(tc.tile_pool(name="wide", bufs=(E - 1) * PASSES - 1))
+        late = ctx.enter_context(tc.tile_pool(name="late", bufs=1))
         psum_sums = ctx.enter_context(tc.psum_pool(name="psum_sums", bufs=3))
         psum_turned = ctx.enter_context(tc.psum_pool(name="psum_turned", bufs=4))
         psum_dx = ctx.enter_context(tc.psum_pool(name="psum_dx", bufs=1))
@@ -60,7 +61,7 @@ def tile_moe_bdx_mlp_relu2_kernel(
         w2_s_first = keep.tile([P, 1, H], U8, name="w2_s_first", align_bytes=64)
         w2_s_rest = keep.tile([P, E - 1, H], U8, name="w2_s_rest", align_bytes=64)
         w2_s = [w2_s_first[:, 0, :]] + [w2_s_rest[:, e, :] for e in range(E - 1)]
-        w1_w = keep.tile([P, E * PASSES, 2 * K], U8, name="w1_w", align_bytes=64)
+        w1_w = {}
         w1_s = keep.tile([P, E * PASSES, K], U8, name="w1_s", align_bytes=64)
         gate_rows = keep.tile([P, P], F32, name="gate_rows")
         gate2 = keep.tile([P, BLOCKS], F32, name="gate2")
@@ -77,7 +78,13 @@ def tile_moe_bdx_mlp_relu2_kernel(
                 queue.dma_start(out=plane[r:P:32].bitcast(I32), in_=rows[r:16:4].bitcast(I32))
 
         def load_a(first, width, s):
-            tile = keep.tile([P, PACK, width], F32, name="a_%d_%d" % (first, s))
+            name = "a_%d_%d" % (first, s)
+            if (first, s) == (S - C, 0):
+                tile = late.tile([P, PACK, width], F32, name=name, tag="late", align_bytes=64)
+            elif width == C:
+                tile = wide.tile([P, PACK, width], F32, name=name, tag="wide")
+            else:
+                tile = keep.tile([P, PACK, width], F32, name=name)
             rows = a[s * PASS : (s + 1) * PASS, first : first + width]
             nc.sync.dma_start(out=tile[:], in_=rows.rearrange("(p t) j -> p t j", t=PACK))
             for u in range(first // UNIT, (first + width) // UNIT):
@@ -85,6 +92,11 @@ def tile_moe_bdx_mlp_relu2_kernel(
 
         def load_w2(queue, e):
             queue.dma_start(out=w2_w[e][:].bitcast(I32), in_=w2_words[e, 0].bitcast(I32))
+
+        def load_w1(pool, tag, kt):
+            w1_w[kt] = pool.tile([P, E * PASSES, 2 * P], U8, name="w1_w%d" % kt, tag=tag, align_bytes=64)
+            words = w1_words.rearrange("e s p c -> p (e s) c")[:, :, 2 * kt * P : 2 * (kt + 1) * P]
+            nc.sync.dma_start(out=w1_w[kt][:].bitcast(I32), in_=words.bitcast(I32))
 
         nc.sync.dma_start(offs_sb[:], offs)
         nc.sync.dma_start(out=dy_w[:], in_=dy_words[0].rearrange("p t d -> p (t d)").bitcast(I32))
@@ -104,9 +116,7 @@ def tile_moe_bdx_mlp_relu2_kernel(
                 load_a(e * C, C, s)
             if e == 1:
                 load_scales(nc.sync, w1_s[:], w1_scales.rearrange("e s f k -> f (e s) k"))
-                nc.sync.dma_start(
-                    out=w1_w[:].bitcast(I32), in_=w1_words.rearrange("e s p c -> p (e s) c").bitcast(I32)
-                )
+                load_w1(keep, "w1_w", 0)
         nc.sync.dma_start(pos_sb[0][:], pos1)
         nc.sync.dma_start(pos_sb[1][:], pos2)
 
@@ -205,12 +215,12 @@ def tile_moe_bdx_mlp_relu2_kernel(
             )
 
         def second_product(e, kt):
-            acc = psum_dx.tile([P, C], F32, name="acc")
+            acc = (psum_dx, psum_sums)[kt].tile([P, C], F32, name="sums")
             for s in range(PASSES):
                 g = e * PASSES + s
                 nc.tensor.matmul_mx(
                     out=acc[:],
-                    lhsT=w1_w[:, g, 2 * kt * P : 2 * (kt + 1) * P].bitcast(E2M1),
+                    lhsT=w1_w[kt][:, g, :].bitcast(E2M1),
                     lhsT_scale=w1_s[:, g, kt * P : (kt + 1) * P],
                     rhs=codes[e][:, s, :].bitcast(E5M2),
                     rhs_scale=scales[e][:, s, :],
@@ -228,36 +238,39 @@ def tile_moe_bdx_mlp_relu2_kernel(
         for n, (u, s) in enumerate(steps):
             multiply = multiply_pair if n < direct_from else multiply_block
             e, place = divmod(n, steps_per_expert)
-            if e > 0 and place >= 2:
-                second_product(e - 1, place - 2)
+            if e > 0 and place == 3:
+                second_product(e - 1, 0)
             if n < last:
                 first_product(n + 1)
-            if 0 <= n - 1 < direct_from:
-                interleave(n - 1)
+            if 0 <= n - 2 < direct_from:
+                interleave(n - 2)
             multiply(n, 0)
             if u + AHEAD < UNITS:
                 (gather_words, gather_scales)[s](u + AHEAD)
             multiply(n, 1)
-            if n >= 2:
-                quantize(n - 2, 0, UNIT)
+            if n >= 3:
+                quantize(n - 3, 0, UNIT)
+        quantize(last - 2, 0, UNIT)
         quantize(last - 1, 0, UNIT)
         for first in (0, P):
             quantize(last, first, P)
-        for kt in range(K_TILES):
-            second_product(E - 1, kt)
+        second_product(E - 1, 0)
+        load_w1(late, "late", 1)
+        for e in range(E):
+            second_product(e, 1)
 
         pieces = [(0, 0, 768), (0, 768, 768), (1, 0, 768), (1, 768, 384), (1, 1152, 384)]
         picked = {}
 
         def pick(n, r):
             kt, first, width = pieces[n]
-            picked[n, r] = combine.tile([P, width], F32, name="picked%d" % r)
+            picked[n, r] = wide.tile([P, width], F32, name="picked%d" % r, tag="wide")
             entries = pos_sb[r][:, first // LANES : (first + width) // LANES]
             nc.vector.tensor_copy(picked[n, r][:], dx[kt][:].indirect(entries))
 
         def add_and_store(n):
             kt, first, width = pieces[n]
-            total = combine.tile([P, width], F32, name="total")
+            total = wide.tile([P, width], F32, name="total", tag="wide")
             engine = nc.vector if n == len(pieces) - 1 else nc.gpsimd
             engine.tensor_tensor(total[:], picked[n, 0][:], picked[n, 1][:], ALU.add)
             nc.sync.dma_start(out=out[kt * P : (kt + 1) * P, first : first + width], in_=total[:])

from contextlib import ExitStack

import concourse.mybir as mybir
from concourse.masks import make_identity

K, T, E, C, H, N = 256, 1536, 6, 512, 1024, 512
S = E * C

FLOPS = 2 * S * (N * H + H * K)
BYTES = (
    4 * H * S + 4 * S + 4 * K * T + N * T + N * T // 32
    + E * (N * H + H * K) // 2 + E * (N * H + H * K) // 32 + 128 * 2 * (S + 2 * T) // 16
)

F32 = mybir.dt.float32
BF16 = mybir.dt.bfloat16
I32 = mybir.dt.int32
U32 = mybir.dt.uint32
U16 = mybir.dt.uint16
U8 = mybir.dt.uint8
E5M2 = mybir.dt.float8_e5m2_x4
E2M1 = mybir.dt.float4_e2m1fn_x4
ALU = mybir.AluOpType
COPY = mybir.ActivationFunctionType.Copy

P = 128
PACK = 4
PASS = P * PACK
PASSES = H // PASS
BLOCKS = S // P
UNIT = 256
UNITS = S // UNIT
AHEAD = 2
DIRECT_STEPS = 2
K_TILES = K // P
LANES = 16


def tile_moe_bdx_mlp_relu2_kernel(
    tc, dy_words, dy_scales, a, w2_words, w2_scales, w1_words, w1_scales, gate, offs, pos1, pos2, out
):
    nc = tc.nc
    with ExitStack() as ctx:
        keep = ctx.enter_context(tc.tile_pool(name="keep", bufs=1))
        gathered = ctx.enter_context(tc.tile_pool(name="gathered", bufs=3))
        paired = ctx.enter_context(tc.tile_pool(name="paired", bufs=4))
        gated = ctx.enter_context(tc.tile_pool(name="gated", bufs=6))
        rounded = ctx.enter_context(tc.tile_pool(name="rounded", bufs=4))
        coded = ctx.enter_context(tc.tile_pool(name="coded", bufs=E))
        wide = ctx.enter_context(tc.tile_pool(name="wide", bufs=(E - 1) * PASSES - 1))
        late = ctx.enter_context(tc.tile_pool(name="late", bufs=1))
        psum_sums = ctx.enter_context(tc.psum_pool(name="psum_sums", bufs=3))
        psum_turned = ctx.enter_context(tc.psum_pool(name="psum_turned", bufs=4))
        psum_dx = ctx.enter_context(tc.psum_pool(name="psum_dx", bufs=1))

        offs_sb = keep.tile([P, S // LANES], U16, name="offs_sb")
        pos_sb = [keep.tile([P, T // LANES], U16, name="pos%d_sb" % (r + 1)) for r in range(2)]
        dy_w = keep.tile([P, T], I32, name="dy_w", align_bytes=64)
        dy_s = keep.tile([P, T], U8, name="dy_s", align_bytes=64)
        w2_w = [keep.tile([P, 2 * H], U8, name="w2_w%d" % e, align_bytes=64) for e in range(E)]
        w2_s_first = keep.tile([P, 1, H], U8, name="w2_s_first", align_bytes=64)
        w2_s_rest = keep.tile([P, E - 1, H], U8, name="w2_s_rest", align_bytes=64)
        w2_s = [w2_s_first[:, 0, :]] + [w2_s_rest[:, e, :] for e in range(E - 1)]
        w1_w = {}
        w1_s = keep.tile([P, E * PASSES, K], U8, name="w1_s", align_bytes=64)
        gate_rows = keep.tile([P, P], F32, name="gate_rows")
        gate2 = keep.tile([P, BLOCKS], F32, name="gate2")
        ident = keep.tile([P, P], F32, name="ident")
        dx = [keep.tile([P, S], F32, name="dx%d" % kt) for kt in range(K_TILES)]
        a_sb = {}

        nc.vector.memset(dy_s[:].bitcast(I32), 0)
        for plane in (w2_s_first, w2_s_rest, w1_s):
            nc.vector.memset(plane[:].rearrange("p g c -> p (g c)").bitcast(I32), 0)

        def load_scales(queue, plane, rows):
            for r in range(4):
                queue.dma_start(out=plane[r:P:32].bitcast(I32), in_=rows[r:16:4].bitcast(I32))

        def load_a(first, width, s):
            name = "a_%d_%d" % (first, s)
            if (first, s) == (S - C, 0):
                tile = late.tile([P, PACK, width], F32, name=name, tag="late", align_bytes=64)
            elif width == C:
                tile = wide.tile([P, PACK, width], F32, name=name, tag="wide")
            else:
                tile = keep.tile([P, PACK, width], F32, name=name)
            rows = a[s * PASS : (s + 1) * PASS, first : first + width]
            nc.sync.dma_start(out=tile[:], in_=rows.rearrange("(p t) j -> p t j", t=PACK))
            for u in range(first // UNIT, (first + width) // UNIT):
                a_sb[u, s] = tile[:, :, u * UNIT - first : (u + 1) * UNIT - first]

        def load_w2(queue, e):
            queue.dma_start(out=w2_w[e][:].bitcast(I32), in_=w2_words[e, 0].bitcast(I32))

        def load_w1(pool, tag, kt):
            w1_w[kt] = pool.tile([P, E * PASSES, 2 * P], U8, name="w1_w%d" % kt, tag=tag, align_bytes=64)
            words = w1_words.rearrange("e s p c -> p (e s) c")[:, :, 2 * kt * P : 2 * (kt + 1) * P]
            nc.sync.dma_start(out=w1_w[kt][:].bitcast(I32), in_=words.bitcast(I32))

        nc.sync.dma_start(offs_sb[:], offs)
        nc.sync.dma_start(out=dy_w[:], in_=dy_words[0].rearrange("p t d -> p (t d)").bitcast(I32))
        load_scales(nc.sync, dy_s[:], dy_scales[0])
        w2_scale_rows = w2_scales.rearrange("e s f i -> f (e s) i")
        nc.sync.dma_start(out=gate_rows[:], in_=gate.rearrange("h (c q) -> (h c) q", q=P)[0:P])
        load_w2(nc.sync, 0)
        load_scales(nc.sync, w2_s_first[:], w2_scale_rows[:, 0:1])
        make_identity(nc, ident[:])
        for first in (0, UNIT):
            for s in range(PASSES):
                load_a(first, UNIT, s)
        load_scales(nc.sync, w2_s_rest[:], w2_scale_rows[:, 1:E])
        for e in range(1, E):
            load_w2(nc.sync, e)
            for s in range(PASSES):
                load_a(e * C, C, s)
            if e == 1:
                load_scales(nc.sync, w1_s[:], w1_scales.rearrange("e s f k -> f (e s) k"))
                load_w1(keep, "w1_w", 0)
        nc.sync.dma_start(pos_sb[0][:], pos1)
        nc.sync.dma_start(pos_sb[1][:], pos2)

        gate_turned = psum_turned.tile([P, 2, UNIT], F32, name="turned")
        nc.tensor.transpose(gate_turned[:, 0, 0:P], gate_rows[:], ident[:])
        nc.scalar.activation(out=gate2[:], in_=gate_turned[:, 0, 0:BLOCKS], func=COPY, scale=2.0)

        g_w, g_s, dh_t, pairs, da, codes, scales = {}, {}, {}, {}, {}, {}, {}
        steps = [(u, s) for u in range(UNITS) for s in range(PASSES)]
        steps_per_expert = len(steps) // E

        def gather_words(u):
            g_w[u] = gathered.tile([P, UNIT], U32, name="g_w", align_bytes=64)
            entries = offs_sb[:, u * UNIT // LANES : (u + 1) * UNIT // LANES]
            nc.vector.tensor_copy(g_w[u][:], dy_w[:].bitcast(U32).indirect(entries))

        def gather_scales(u):
            g_s[u] = gathered.tile([P, UNIT], U8, name="g_s", align_bytes=64)
            entries = offs_sb[:, u * UNIT // LANES : (u + 1) * UNIT // LANES]
            nc.vector.tensor_copy(g_s[u][:], dy_s[:].indirect(entries))

        def first_product(n):
            u, s = steps[n]
            e = u * UNIT // C
            for b in range(UNIT // P):
                slots = slice(b * P, (b + 1) * P)
                j = u * UNIT // P + b
                sums = psum_sums.tile([P, PASS], F32, name="sums")
                nc.tensor.matmul_mx(
                    out=sums[:],
                    lhsT=g_w[u][:, slots].bitcast(E5M2),
                    lhsT_scale=g_s[u][:, slots],
                    rhs=w2_w[e][:, 2 * s * PASS : 2 * (s + 1) * PASS].bitcast(E2M1),
                    rhs_scale=w2_s[e][:, s * PASS : (s + 1) * PASS],
                    start=True,
                    stop=True,
                )
                dh_t[n, b] = gated.tile([P, PACK, P], F32, name="dh_t")
                nc.scalar.activation(
                    out=dh_t[n, b][:],
                    in_=sums[:].rearrange("p (m t) -> p t m", t=PACK),
                    func=COPY,
                    scale=gate2[:, j : j + 1],
                )

        def relu_times(result, a_part, turned):
            nc.vector.scalar_tensor_tensor(
                out=result,
                in0=a_part.rearrange("p t n -> p n t"),
                scalar=0.0,
                in1=turned.rearrange("p t n -> p n t"),
                op0=ALU.max,
                op1=ALU.mult,
            )

        def multiply_pair(n, half):
            if half == 0:
                pairs[n] = paired.tile([P, 2, UNIT, 2], BF16, name="pairs", align_bytes=64)
            turned = psum_turned.tile([P, 2, UNIT], F32, name="turned")
            for b in range(UNIT // P):
                for d in range(2):
                    nc.tensor.transpose(turned[:, d, b * P : (b + 1) * P], dh_t[n, b][:, 2 * half + d, :], ident[:])
            relu_times(pairs[n][:, half], a_sb[steps[n]][:, 2 * half : 2 * half + 2, :], turned[:])

        def interleave(n):
            da[n] = rounded.tile([P, UNIT * PACK], BF16, name="da", align_bytes=64)
            copy = nc.vector.tensor_copy if n % 4 == 4-1 else nc.scalar.copy
            copy(
                out=da[n][:].bitcast(F32).rearrange("p (n h) -> p n h", h=2),
                in_=pairs[n][:].rearrange("p h n d -> p h (n d)").bitcast(F32).rearrange("p h n -> p n h"),
            )

        def multiply_block(n, b):
            if b == 0:
                da[n] = rounded.tile([P, UNIT * PACK], BF16, name="da", align_bytes=64)
            turned = psum_turned.tile([P, PACK, P], F32, name="turned")
            for t in range(PACK):
                nc.tensor.transpose(turned[:, t, :], dh_t[n, b][:, t, :], ident[:])
            relu_times(
                da[n][:, b * P * PACK : (b + 1) * P * PACK].rearrange("p (n t) -> p n t", t=PACK),
                a_sb[steps[n]][:, :, b * P : (b + 1) * P],
                turned[:],
            )

        def quantize(n, first, width):
            u, s = steps[n]
            e = u * UNIT // C
            if e not in codes:
                codes[e] = coded.tile([P, PASSES, C], U32, name="codes", align_bytes=64)
                scales[e] = coded.tile([P, PASSES, C], U8, name="scales", align_bytes=64)
            slots = slice(u * UNIT % C + first, u * UNIT % C + first + width)
            nc.vector.quantize_mx(
                out=codes[e][:, s, slots].bitcast(E5M2),
                scales=scales[e][:, s, slots],
                in_=da[n][:, first * PACK : (first + width) * PACK],
            )

        def second_product(e, kt):
            acc = (psum_dx, psum_sums)[kt].tile([P, C], F32, name="sums")
            for s in range(PASSES):
                g = e * PASSES + s
                nc.tensor.matmul_mx(
                    out=acc[:],
                    lhsT=w1_w[kt][:, g, :].bitcast(E2M1),
                    lhsT_scale=w1_s[:, g, kt * P : (kt + 1) * P],
                    rhs=codes[e][:, s, :].bitcast(E5M2),
                    rhs_scale=scales[e][:, s, :],
                    start=(s == 0),
                    stop=(s == PASSES - 1),
                )
            nc.scalar.copy(out=dx[kt][:, e * C : (e + 1) * C], in_=acc[:])

        last = len(steps) - 1
        direct_from = len(steps) - DIRECT_STEPS
        for u in range(AHEAD):
            gather_words(u)
            gather_scales(u)
        first_product(0)
        for n, (u, s) in enumerate(steps):
            multiply = multiply_pair if n < direct_from else multiply_block
            e, place = divmod(n, steps_per_expert)
            if e > 0 and place == 3:
                second_product(e - 1, 0)
            if n < last:
                first_product(n + 1)
            if 0 <= n - 2 < direct_from:
                interleave(n - 2)
            multiply(n, 0)
            if u + AHEAD < UNITS:
                (gather_words, gather_scales)[s](u + AHEAD)
            multiply(n, 1)
            if n >= 3:
                quantize(n - 3, 0, UNIT)
        quantize(last - 2, 0, UNIT)
        quantize(last - 1, 0, UNIT)
        for first in (0, P):
            quantize(last, first, P)
        second_product(E - 1, 0)
        load_w1(late, "late", 1)
        for e in range(E):
            second_product(e, 1)

        pieces = [(0, 0, 768), (0, 768, 768), (1, 0, 768), (1, 768, 384), (1, 1152, 384)]
        picked = {}

        def pick(n, r):
            kt, first, width = pieces[n]
            picked[n, r] = wide.tile([P, width], F32, name="picked%d" % r, tag="wide")
            entries = pos_sb[r][:, first // LANES : (first + width) // LANES]
            nc.vector.tensor_copy(picked[n, r][:], dx[kt][:].indirect(entries))

        def add_and_store(n):
            kt, first, width = pieces[n]
            total = wide.tile([P, width], F32, name="total", tag="wide")
            engine = nc.vector if n == len(pieces) - 1 else nc.gpsimd
            engine.tensor_tensor(total[:], picked[n, 0][:], picked[n, 1][:], ALU.add)
            nc.sync.dma_start(out=out[kt * P : (kt + 1) * P, first : first + width], in_=total[:])

        for n in range(len(pieces)):
            pick(n, 0)
            if n > 0:
                add_and_store(n - 1)
            pick(n, 1)
        add_and_store(len(pieces) - 1)
